import numpy as np
import ml_dtypes


def mxq(x, axis, fmt="e4m3"):
    dtype, down = {"e4m3": (ml_dtypes.float8_e4m3fn, 7), "e5m2": (ml_dtypes.float8_e5m2, 14)}[fmt]
    v = np.moveaxis(np.asarray(x, np.float32).astype(ml_dtypes.bfloat16).astype(np.float64), axis, -1)
    blocks = v.reshape(v.shape[:-1] + (-1, 32))
    amax = np.abs(blocks).max(-1, keepdims=True)
    byte = np.maximum(np.where(amax > 0, np.frexp(amax)[1] - 1 + 127, 0) - down, 1)
    scale = np.exp2(byte - 127.0)
    codes = (blocks / scale).astype(np.float32).astype(dtype).astype(np.float64)
    return np.moveaxis((codes * scale).reshape(v.shape), -1, axis)


WIDE = False


def mx_kscale(k):
    if not WIDE:
        return np.ones(k)
    levels = np.array([10, -10, 5, -5, 0])
    if k % 512:
        return np.exp2(np.random.permutation(np.resize(levels, k // 32))).repeat(32)
    a = np.empty((k // 512, 16))
    for p in range(k // 512):
        a[p, :8] = np.random.permutation(np.resize(levels, 8))
        for g in range(8):
            far = levels[np.abs(levels - a[p, g]) >= 10]
            a[p, g + 8] = far[np.random.randint(len(far))]
    return np.exp2(a.ravel()).repeat(32)


def f64(x):
    return np.asarray(x).astype(np.float64)


def striped(idx):
    return np.tile(idx.reshape(-1, 16).T, (8, 1)).astype(np.uint16)


def unstriped(offs):
    return offs[:16].T.reshape(-1).astype(np.int64)


E2M1 = np.array([0.0, 0.5, 1.0, 1.5, 2.0, 3.0, 4.0, 6.0, -0.0, -0.5, -1.0, -1.5, -2.0, -3.0, -4.0, -6.0])


def pack_weight(w, fmt):
    k, n = w.shape
    w = f64(np.asarray(w, np.float32).astype(ml_dtypes.bfloat16)).reshape(k // 32, 32, n)
    amax = np.abs(w).max(1)
    if fmt == "e4m3":
        byte = np.frexp(amax)[1] - 1 + 127 - 7
    else:
        mant, ex = np.frexp(amax / 6.0)
        byte = np.where(mant > 0.5, ex, ex - 1) + 127
    byte = np.clip(np.where(amax > 0, byte, 1), 1, 254)
    scaled = (w * np.exp2(127.0 - byte)[:, None, :]).reshape(k, n).astype(np.float32)
    by_word = np.ascontiguousarray(scaled.reshape(k // 512, 128, 4, n).transpose(0, 1, 3, 2))
    if fmt == "e4m3":
        words = by_word.astype(ml_dtypes.float8_e4m3fn).view(np.uint8)
    else:
        c = by_word.astype(ml_dtypes.float4_e2m1fn).view(np.uint8) & 0xF
        words = (c[..., 0::2] | (c[..., 1::2] << 4)).reshape(k // 512, 128, 2 * n)
    return np.ascontiguousarray(words), np.ascontiguousarray(byte.astype(np.uint8).reshape(k // 512, 16, n))


def unpack_weight(words, scales, fmt):
    g, _, n = scales.shape
    words = np.ascontiguousarray(words).reshape(g, 128, n, -1)
    if fmt == "e4m3":
        vals = words.view(ml_dtypes.float8_e4m3fn).astype(np.float64)
    else:
        nib = np.empty((g, 128, n, 4), np.uint8)
        nib[..., 0::2] = words & 0xF
        nib[..., 1::2] = words >> 4
        vals = E2M1[nib]
    vals = vals * np.repeat(np.exp2(scales.astype(np.float64) - 127.0), 8, axis=1)[..., None]
    return vals.transpose(0, 1, 3, 2).reshape(g * 512, n)


def gelu(v):
    return 0.5 * v * (1.0 + np.tanh(np.sqrt(2.0 / np.pi) * (v + 0.044715 * v**3)))


def striped8(idx):
    return np.concatenate([v.reshape(-1, 16).T for v in idx]).astype(np.uint16)


def unstriped8(offs):
    return np.stack([offs[16 * g:16 * g + 16].T.reshape(-1) for g in range(8)]).astype(np.int64)


def runs(v, idx8):
    k = np.arange(v.shape[0])
    return v[k[:, None], idx8[k % 512 // 64]]


K, K2, H, N, T, S, T2 = 1024, 512, 1024, 512, 2048, 1024, 2048

def setup_inputs():
    n = np.random.standard_normal
    s = mx_kscale(K)[:, None]
    s2 = mx_kscale(K2)[:, None]
    u = mx_kscale(H)[:, None]
    tab_words, tab_scales = pack_weight(n((K, T)) * s, "e4m3")
    tab2_words, tab2_scales = pack_weight(n((K2, T)) * s2, "e4m3")
    w4_words, w4_scales = pack_weight(n((K2, H)) / np.sqrt(K2) / s2, "e2m1")
    return {
        "tab_words": tab_words, "tab_scales": tab_scales,
        "tab2_words": tab2_words, "tab2_scales": tab2_scales,
        "offs": striped8(np.stack([np.random.permutation(T)[:S] for _ in range(8)])),
        "offs2": striped(np.random.permutation(T)[:S]),
        "offs3": striped(np.random.permutation(T2)[:S]),
        "w1": (n((K, H)) / np.sqrt(K) / s).astype(np.float32),
        "w4_words": w4_words, "w4_scales": w4_scales,
        "stiff": np.exp(0.4 * n(H)).astype(np.float32),
        "reach": (np.exp(0.3 * n(H)) * u[:, 0]).astype(np.float32),
        "w2": (n((H, N)) / np.sqrt(H) / u).astype(np.float32),
        "page1": n((N, T2)).astype(np.float32),
        "wgo": np.exp(0.3 * n((128, S))).astype(np.float32),
    }

def reference(tab_words, tab_scales, tab2_words, tab2_scales, offs, offs2, offs3,
              w1, w4_words, w4_scales, stiff, reach, w2, page1, wgo):
    v = runs(unpack_weight(tab_words, tab_scales, "e4m3"), unstriped8(offs))
    v2 = unpack_weight(tab2_words, tab2_scales, "e4m3")[:, unstriped(offs2)]
    w4 = unpack_weight(w4_words, w4_scales, "e2m1")
    pluck = mxq(f64(w1), 0, "e4m3").T @ v
    quill = w4.T @ v2
    bent = np.tanh(f64(stiff)[:, None] * pluck + quill)
    h = f64(reach)[:, None] * bent
    y = mxq(f64(w2), 0, "e4m3").T @ mxq(h, 0, "e4m3")
    out = f64(page1).copy()
    out[:, unstriped(offs3)] = np.tile(f64(wgo), (N // 128, 1)) * y
    return out

@@ -1,0 +1,307 @@
+from contextlib import ExitStack
+
+import concourse.mybir as mybir
+
+K, K2, H, N, T, S, T2 = 1024, 512, 1024, 512, 2048, 1024, 2048
+FLOPS = 2 * S * H * (K + K2 + N)
+
+F32 = mybir.dt.float32
+BF16 = mybir.dt.bfloat16
+I32 = mybir.dt.int32
+U32 = mybir.dt.uint32
+U16 = mybir.dt.uint16
+U8 = mybir.dt.uint8
+FP8X4 = mybir.dt.float8_e4m3fn_x4
+FP4X4 = mybir.dt.float4_e2m1fn_x4
+MULT = mybir.AluOpType.mult
+ADD = mybir.AluOpType.add
+TANH = mybir.ActivationFunctionType.Tanh
+
+P = 128
+PACK = 4
+PASS = P * PACK
+W = 256
+CHUNKS = S // W
+GATHER = 512
+
+
+def tile_list_plectrum_voicing_scorer_kernel(
+    tc, tab_words, tab_scales, tab2_words, tab2_scales, offs, offs2, offs3,
+    w1, w4_words, w4_scales, stiff, reach, w2, page1, wgo, out,
+):
+    nc = tc.nc
+    with ExitStack() as ctx:
+        keep = ctx.enter_context(tc.tile_pool(name="keep", bufs=1))
+        ring = ctx.enter_context(tc.tile_pool(name="ring", bufs=3))
+        psum = ctx.enter_context(tc.psum_pool(name="psum", bufs=1))
+
+        def held(shape, dtype, name):
+            return keep.tile(shape, dtype, name=name, align_bytes=64)
+
+        list1 = keep.tile([P, S // 16], U16, name="list1")
+        list2 = keep.tile([P, S // 16], U16, name="list2")
+        list3 = keep.tile([P, S // 16], U16, name="list3")
+        def slot(shape, dtype, name, tag):
+            return keep.tile(shape, dtype, name=name, tag=tag, align_bytes=64)
+
+        tab_sb = {0: slot([P, T], I32, "tab_sb0", "D")}
+        tabs_sb = slot([P, T], U8, "tabs_sb", "C")
+        tab2s_sb = held([P, T], U8, "tab2s_sb")
+        w4_raw = slot([P, 2 * H], U8, "w4_raw", "B")
+        w4s_raw = held([P, H], U8, "w4s_raw")
+        w1_raw, w2_raw, page, late = {}, {}, {}, {}
+        stiff_sb = held([P, 2, PACK], F32, "stiff_sb")
+        reach_sb = held([P, 2, PACK], F32, "reach_sb")
+
+        def words(dram):
+            return dram.rearrange("p t i -> p (t i)").bitcast(I32)
+
+        def load_w2(r, tag):
+            w2_raw[r] = slot([P, PACK, N], F32, "w2_raw%d" % r, tag)
+            nc.sync.dma_start(w2_raw[r][:], w2[r * PASS:(r + 1) * PASS, :].rearrange("(p i) n -> p i n", i=PACK))
+
+        def load_page(nt, tag):
+            page[nt] = slot([P, T2], F32, "page%d" % nt, tag)
+            nc.sync.dma_start(page[nt][:], page1[nt * P:(nt + 1) * P, :])
+
+        def load_w1(a, r, tag):
+            w1_raw[a, r] = slot([P, PACK, PASS], F32, "w1_raw%d%d" % (a, r), tag)
+            nc.sync.dma_start(
+                w1_raw[a, r][:],
+                w1[a * PASS:(a + 1) * PASS, r * PASS:(r + 1) * PASS].rearrange("(p i) c -> p i c", i=PACK),
+            )
+
+        def load_scale_rows(plane, rows):
+            nc.vector.memset(plane[:].bitcast(I32), 0)
+            for q in range(4):
+                nc.scalar.dma_start(plane[32 * q:32 * q + 4, :].bitcast(I32), rows[4 * q:4 * q + 4, :].bitcast(I32))
+
+        nc.sync.dma_start(list1[:], offs)
+        nc.sync.dma_start(list2[:], offs2)
+        nc.sync.dma_start(list3[:], offs3)
+        nc.scalar.dma_start(stiff_sb[:], stiff.rearrange("(r p t) -> p r t", p=P, t=PACK))
+        nc.scalar.dma_start(reach_sb[:], reach.rearrange("(r p t) -> p r t", p=P, t=PACK))
+        nc.sync.dma_start(w4_raw[:].bitcast(I32), w4_words[0].bitcast(I32))
+        nc.sync.dma_start(tab_sb[0][:], words(tab_words[0]))
+        load_w1(0, 0, "A")
+
+        nc.vector.memset(tabs_sb[:].bitcast(I32), 0)
+        for a in range(2):
+            for e in range(2):
+                nc.scalar.dma_start(tabs_sb[4 * a + e:P:16, :].bitcast(I32), tab_scales[a, e:16:2, :].bitcast(I32))
+
+        vs_picked = held([P, S], U8, "vs_picked")
+        v_scale = held([P, S], U8, "v_scale")
+        v_first = held([P, S], U32, "v_first")
+        v = {(0, g): v_first[:, g * GATHER:(g + 1) * GATHER] for g in range(2)}
+        v2, v2_scale = {}, {}
+
+        def gather(dst, window, offsets, g):
+            cols = slice(g * GATHER // 16, (g + 1) * GATHER // 16)
+            nc.vector.tensor_copy(dst, window.indirect(offsets[:, cols]))
+
+        w4_codes = held([P, 2 * H], U8, "w4_codes")
+        w4_scale = held([P, H], U8, "w4_scale")
+        nc.vector.tensor_copy(
+            w4_codes[:].bitcast(U16).rearrange("p (r t m) -> p r m t", r=2, t=PACK),
+            w4_raw[:].bitcast(U16).rearrange("p (r m t) -> p r m t", r=2, t=PACK),
+        )
+        tab_sb[1] = slot([P, T], I32, "tab_sb1", "B")
+        nc.sync.dma_start(tab_sb[1][:], words(tab_words[1]))
+        load_scale_rows(tab2s_sb, tab2_scales[0])
+        load_scale_rows(w4s_raw, w4_scales[0])
+        nc.vector.tensor_copy(vs_picked[:], tabs_sb[:].indirect(list1[:]))
+        load_w1(1, 0, "C")
+        nc.vector.tensor_copy(v_scale[:].bitcast(I32), vs_picked[:].bitcast(I32))
+        nc.vector.tensor_copy(v_first[:], tab_sb[0][:].bitcast(U32).indirect(list1[:]))
+
+        w1_codes = {(a, r): held([P, PASS], U32, "w1_codes%d%d" % (a, r)) for a in range(2) for r in range(2)}
+        w1_scale = {(a, r): held([P, PASS], U8, "w1_scale%d%d" % (a, r)) for a in range(2) for r in range(2)}
+        w2_codes = [held([P, N], U32, "w2_codes%d" % r) for r in range(2)]
+        w2_scale = [held([P, N], U8, "w2_scale%d" % r) for r in range(2)]
+
+        def quantise(codes, scale, rounded):
+            nc.vector.quantize_mx(out=codes.bitcast(FP8X4), scales=scale, in_=rounded)
+
+        def make_w1(a, r, tag, pieces):
+            rounded = keep.tile([P, PACK * PASS], BF16, name="w1_rounded%d%d" % (a, r), tag=tag, align_bytes=64)
+            dst = rounded[:].rearrange("p (t m i) -> p m i t", t=PACK, i=PACK)
+            src = w1_raw[a, r][:].rearrange("p i (m t) -> p m i t", t=PACK)
+            for piece in range(pieces):
+                m = slice(piece * P // pieces, (piece + 1) * P // pieces)
+                nc.scalar.copy(dst[:, m], src[:, m])
+            quantise(w1_codes[a, r][:], w1_scale[a, r][:], rounded[:])
+
+        def make_w2(r, tag, on_vector):
+            rounded = keep.tile([P, PACK * N], BF16, name="w2_rounded%d" % r, tag=tag, align_bytes=64)
+            dst = rounded[:].rearrange("p (m e i) -> p m i e", e=4, i=PACK)
+            src = w2_raw[r][:].rearrange("p i (m e) -> p m i e", e=4)
+            if on_vector:
+                nc.vector.tensor_copy(dst, src)
+            else:
+                for piece in range(4):
+                    m = slice(piece * P // 4, (piece + 1) * P // 4)
+                    nc.scalar.copy(dst[:, m], src[:, m])
+            quantise(w2_codes[r][:], w2_scale[r][:], rounded[:])
+
+        def gather_tab(g, tag):
+            t = keep.tile([P, GATHER], U32, name="v1%d" % g, tag=tag, align_bytes=64)
+            gather(t[:], tab_sb[1][:].bitcast(U32), list1, g)
+            v[1, g] = t[:]
+
+        def gather_tab2(g, tag):
+            t = keep.tile([P, GATHER], U32, name="v2%d" % g, tag=tag, align_bytes=64)
+            gather(t[:], tab2_sb[:].bitcast(U32), list2, g)
+            v2[g] = t[:]
+
+        def gather_tab2_scales(g, tag):
+            t = keep.tile([P, GATHER], U8, name="v2_scale%d" % g, tag=tag, align_bytes=64)
+            gather(t[:], tab2s_sb[:], list2, g)
+            v2_scale[g] = t[:]
+
+        make_w1(0, 0, "w1_rounded00", 1)
+        for a in range(2):
+            for e in range(2):
+                nc.sync.dma_start(
+                    v_scale[4 * a + 2 + e:P:32, :].bitcast(I32), vs_picked[16 + 4 * a + e:P:32, :].bitcast(I32)
+                )
+        load_w1(0, 1, "D")
+        tab2_sb = slot([P, T], I32, "tab2_sb", "A")
+        nc.sync.dma_start(tab2_sb[:], words(tab2_words[0]))
+        for g in range(2):
+            gather_tab(g, "v1%d" % g)
+        load_w1(1, 1, "B")
+        for g in range(2):
+            gather_tab2_scales(g, "v2_scale%d" % g)
+        make_w1(1, 0, "w1_rounded10", 1)
+        load_w2(0, "C")
+        nc.vector.tensor_copy(
+            w4_scale[:].rearrange("p (r t m) -> p r m t", r=2, t=PACK),
+            w4s_raw[:].rearrange("p (r m t) -> p r m t", r=2, t=PACK),
+        )
+        for g in range(2):
+            gather_tab2(g, "v2%d" % g)
+        make_w1(0, 1, "G", 2)
+        load_w2(1, "D")
+        load_page(0, "A")
+        late["wgo"] = slot([P, S], F32, "wgo_sb", "G")
+        nc.sync.dma_start(late["wgo"][:], wgo)
+
+        halves = [held([P, GATHER], U32, "h_codes%d" % j) for j in range(4)]
+        half_scales = [held([P, GATHER], U8, "h_scale%d" % j) for j in range(4)]
+        PER_BANK = 512 // W
+        pre = {}
+        STAGE_DEPTH = 4
+        stage_ring = [held([P, 512], F32, "stage%d" % j) for j in range(STAGE_DEPTH)]
+        stage_used = []
+
+        def next_stage():
+            stage_used.append(0)
+            return stage_ring[(len(stage_used) - 1) % STAGE_DEPTH]
+
+        def inside(c):
+            g = c * W // GATHER
+            return g, slice(c * W - g * GATHER, (c + 1) * W - g * GATHER)
+
+        def first_stage(c, r):
+            g, ins = inside(c)
+            cols = slice(c * W, (c + 1) * W)
+            z = ring.tile([P, PACK, W], F32, name="z")
+            for t0 in range(0, PACK, PER_BANK):
+                pluck = psum.tile([P, PER_BANK, W], F32, name="pluck", bufs=3)
+                quill = psum.tile([P, PER_BANK, W], F32, name="quill", bufs=3)
+                for s in range(PER_BANK):
+                    m0 = (PACK * r + t0 + s) * P
+                    nc.tensor.matmul_mx(
+                        out=quill[:, s, :],
+                        lhsT=w4_codes[:, 2 * m0:2 * (m0 + P)].bitcast(FP4X4), lhsT_scale=w4_scale[:, m0:m0 + P],
+                        rhs=v2[g][:, ins].bitcast(FP8X4), rhs_scale=v2_scale[g][:, ins],
+                        start=True, stop=True,
+                    )
+                for s in range(PER_BANK):
+                    m = slice((t0 + s) * P, (t0 + s + 1) * P)
+                    for a in range(2):
+                        nc.tensor.matmul_mx(
+                            out=pluck[:, s, :],
+                            lhsT=w1_codes[a, r][:, m].bitcast(FP8X4), lhsT_scale=w1_scale[a, r][:, m],
+                            rhs=v[a, g][:, ins].bitcast(FP8X4), rhs_scale=v_scale[4 * a:P, cols],
+                            start=(a == 0), stop=(a == 1),
+                        )
+                quill_sb = next_stage()
+                nc.scalar.copy(quill_sb[:], quill[:].rearrange("p s n -> p (s n)"))
+                for s in range(PER_BANK):
+                    t = t0 + s
+                    nc.vector.scalar_tensor_tensor(
+                        z[:, t, :], pluck[:, s, :], stiff_sb[:, r, t:t + 1], quill_sb[:, s * W:(s + 1) * W], MULT, ADD
+                    )
+            pre[c, r] = z
+
+        def activate(c, r):
+            z = pre[c, r]
+            bent = ring.tile([P, W, PACK], F32, name="bent")
+            nc.scalar.activation(
+                bent[:].rearrange("p (m e) t -> p m t e", e=4), z[:].rearrange("p t (m e) -> p m t e", e=4), TANH
+            )
+            h = ring.tile([P, W, PACK], BF16, name="h", align_bytes=64)
+            nc.vector.tensor_tensor(h[:], bent[:], reach_sb[:, r:r + 1, :].to_broadcast([P, W, PACK]), MULT)
+            pre[c, r] = h
+
+        def quantise_h(c, r):
+            g, ins = inside(c)
+            quantise(halves[2 * g + r][:, ins], half_scales[2 * g + r][:, ins], pre[c, r][:].rearrange("p n t -> p (n t)"))
+
+        def second_stage(g, ins, tiles, last):
+            width = ins.stop - ins.start
+            j0 = g * GATHER + ins.start
+            y = psum.tile([P, 512], F32, name="y", bufs=2)
+            for s, nt in enumerate(tiles):
+                m = slice(nt * P, (nt + 1) * P)
+                for r in range(2):
+                    nc.tensor.matmul_mx(
+                        out=y[:, s * width:(s + 1) * width],
+                        lhsT=w2_codes[r][:, m].bitcast(FP8X4), lhsT_scale=w2_scale[r][:, m],
+                        rhs=halves[2 * g + r][:, ins].bitcast(FP8X4), rhs_scale=half_scales[2 * g + r][:, ins],
+                        start=(r == 0), stop=(r == 1),
+                    )
+            y_sb = next_stage()
+            nc.scalar.copy(y_sb[:, :len(tiles) * width], y[:, :len(tiles) * width])
+            for s, nt in enumerate(tiles):
+                nc.vector.tensor_tensor(
+                    page[nt][:].indirect(list3[:, j0 // 16:(j0 + width) // 16]),
+                    y_sb[:, s * width:(s + 1) * width], late["wgo"][:, j0:j0 + width], MULT,
+                )
+                if last:
+                    nc.sync.dma_start(out[nt * P:(nt + 1) * P, :], page[nt][:])
+
+        def place(c, nt, last=False):
+            g, ins = inside(c)
+            second_stage(g, ins, [nt], last)
+
+        units = [(0, 0), (1, 0), (0, 1), (1, 1), (2, 0), (2, 1), (3, 0), (3, 1)]
+        waiting = [(0, 0), (0, 1), (0, 2), (0, 3), (1, 0), (1, 1), (1, 2), (1, 3)]
+        per_step = [0, 0, 0, 0, 2, 2, 2, 2]
+        for i, unit in enumerate(units):
+            first_stage(*unit)
+            if i > 0:
+                activate(*units[i - 1])
+            if i == 0:
+                make_w1(1, 1, "w1_rounded11", 4)
+                load_page(1, "B")
+            if i == 1:
+                make_w2(0, "w2_rounded0", True)
+                load_page(2, "C")
+            if i == 2:
+                make_w2(1, "w2_rounded1", False)
+                load_page(3, "D")
+            for k in range(per_step[i]):
+                place(*waiting.pop(0))
+            if i > 0:
+                quantise_h(*units[i - 1])
+        place(2, 0)
+        activate(*units[-1])
+        quantise_h(*units[-1])
+        place(2, 1)
+        place(3, 0, True)
+        place(3, 1, True)
+        for nt in range(2, N // P):
+            second_stage(1, slice(0, GATHER), [nt], True)

@@ -20,9 +20,9 @@ TANH = mybir.ActivationFunctionType.Tanh
 P = 128
 PACK = 4
 PASS = P * PACK
-W = 256
-CHUNKS = S // W
 GATHER = 512
+PIECE = 256
+COPY = mybir.ActivationFunctionType.Copy
 
 
 def tile_list_plectrum_voicing_scorer_kernel(
@@ -44,10 +44,10 @@ def tile_list_plectrum_voicing_scorer_kernel(
         def slot(shape, dtype, name, tag):
             return keep.tile(shape, dtype, name=name, tag=tag, align_bytes=64)
 
-        tab_sb = {0: slot([P, T], I32, "tab_sb0", "D")}
-        tabs_sb = slot([P, T], U8, "tabs_sb", "C")
+        tab_sb = [held([P, T], I32, "tab_sb0"), slot([P, T], I32, "tab_sb1", "B")]
+        tabs_sb = held([P, T], U8, "tabs_sb")
+        w4_raw = held([P, 2 * H], U8, "w4_raw")
         tab2s_sb = held([P, T], U8, "tab2s_sb")
-        w4_raw = slot([P, 2 * H], U8, "w4_raw", "B")
         w4s_raw = held([P, H], U8, "w4s_raw")
         w1_raw, w2_raw, page, late = {}, {}, {}, {}
         stiff_sb = held([P, 2, PACK], F32, "stiff_sb")
@@ -74,21 +74,25 @@ def tile_list_plectrum_voicing_scorer_kernel(
         def load_scale_rows(plane, rows):
             nc.vector.memset(plane[:].bitcast(I32), 0)
             for q in range(4):
-                nc.scalar.dma_start(plane[32 * q:32 * q + 4, :].bitcast(I32), rows[4 * q:4 * q + 4, :].bitcast(I32))
+                nc.sync.dma_start(plane[32 * q:32 * q + 4, :].bitcast(I32), rows[4 * q:4 * q + 4, :].bitcast(I32))
 
         nc.sync.dma_start(list1[:], offs)
+        nc.sync.dma_start(tab_sb[0][:], words(tab_words[0]))
+        nc.sync.dma_start(w4_raw[:].bitcast(I32), w4_words[0].bitcast(I32))
         nc.sync.dma_start(list2[:], offs2)
         nc.sync.dma_start(list3[:], offs3)
-        nc.scalar.dma_start(stiff_sb[:], stiff.rearrange("(r p t) -> p r t", p=P, t=PACK))
-        nc.scalar.dma_start(reach_sb[:], reach.rearrange("(r p t) -> p r t", p=P, t=PACK))
-        nc.sync.dma_start(w4_raw[:].bitcast(I32), w4_words[0].bitcast(I32))
-        nc.sync.dma_start(tab_sb[0][:], words(tab_words[0]))
+        nc.sync.dma_start(stiff_sb[:], stiff.rearrange("(r p t) -> p r t", p=P, t=PACK))
+        nc.sync.dma_start(reach_sb[:], reach.rearrange("(r p t) -> p r t", p=P, t=PACK))
         load_w1(0, 0, "A")
-
         nc.vector.memset(tabs_sb[:].bitcast(I32), 0)
         for a in range(2):
             for e in range(2):
-                nc.scalar.dma_start(tabs_sb[4 * a + e:P:16, :].bitcast(I32), tab_scales[a, e:16:2, :].bitcast(I32))
+                nc.sync.dma_start(tabs_sb[4 * a + e:P:16, :].bitcast(I32), tab_scales[a, e:16:2, :].bitcast(I32))
+        nc.sync.dma_start(tab_sb[1][:], words(tab_words[1]))
+        load_scale_rows(tab2s_sb, tab2_scales[0])
+        load_w1(1, 0, "C")
+        load_scale_rows(w4s_raw, w4_scales[0])
+        load_w1(0, 1, "D")
 
         vs_picked = held([P, S], U8, "vs_picked")
         v_scale = held([P, S], U8, "v_scale")
@@ -106,14 +110,9 @@ def tile_list_plectrum_voicing_scorer_kernel(
             w4_codes[:].bitcast(U16).rearrange("p (r t m) -> p r m t", r=2, t=PACK),
             w4_raw[:].bitcast(U16).rearrange("p (r m t) -> p r m t", r=2, t=PACK),
         )
-        tab_sb[1] = slot([P, T], I32, "tab_sb1", "B")
-        nc.sync.dma_start(tab_sb[1][:], words(tab_words[1]))
-        load_scale_rows(tab2s_sb, tab2_scales[0])
-        load_scale_rows(w4s_raw, w4_scales[0])
-        nc.vector.tensor_copy(vs_picked[:], tabs_sb[:].indirect(list1[:]))
-        load_w1(1, 0, "C")
-        nc.vector.tensor_copy(v_scale[:].bitcast(I32), vs_picked[:].bitcast(I32))
         nc.vector.tensor_copy(v_first[:], tab_sb[0][:].bitcast(U32).indirect(list1[:]))
+        nc.vector.tensor_copy(vs_picked[:], tabs_sb[:].indirect(list1[:]))
+        nc.vector.tensor_copy(v_scale[:].bitcast(I32), vs_picked[:].bitcast(I32))
 
         w1_codes = {(a, r): held([P, PASS], U32, "w1_codes%d%d" % (a, r)) for a in range(2) for r in range(2)}
         w1_scale = {(a, r): held([P, PASS], U8, "w1_scale%d%d" % (a, r)) for a in range(2) for r in range(2)}
@@ -165,14 +164,17 @@ def tile_list_plectrum_voicing_scorer_kernel(
                 nc.sync.dma_start(
                     v_scale[4 * a + 2 + e:P:32, :].bitcast(I32), vs_picked[16 + 4 * a + e:P:32, :].bitcast(I32)
                 )
-        load_w1(0, 1, "D")
         tab2_sb = slot([P, T], I32, "tab2_sb", "A")
         nc.sync.dma_start(tab2_sb[:], words(tab2_words[0]))
+        v_second = held([P, S], U32, "v_second")
+        nc.vector.tensor_copy(v_second[:], tab_sb[1][:].bitcast(U32).indirect(list1[:]))
         for g in range(2):
-            gather_tab(g, "v1%d" % g)
+            v[1, g] = v_second[:, g * GATHER:(g + 1) * GATHER]
         load_w1(1, 1, "B")
+        v2s = held([P, S], U8, "v2s")
+        nc.vector.tensor_copy(v2s[:], tab2s_sb[:].indirect(list2[:]))
         for g in range(2):
-            gather_tab2_scales(g, "v2_scale%d" % g)
+            v2_scale[g] = v2s[:, g * GATHER:(g + 1) * GATHER]
         make_w1(1, 0, "w1_rounded10", 1)
         load_w2(0, "C")
         nc.vector.tensor_copy(
@@ -181,127 +183,128 @@ def tile_list_plectrum_voicing_scorer_kernel(
         )
         for g in range(2):
             gather_tab2(g, "v2%d" % g)
-        make_w1(0, 1, "G", 2)
-        load_w2(1, "D")
-        load_page(0, "A")
-        late["wgo"] = slot([P, S], F32, "wgo_sb", "G")
-        nc.sync.dma_start(late["wgo"][:], wgo)
 
-        halves = [held([P, GATHER], U32, "h_codes%d" % j) for j in range(4)]
-        half_scales = [held([P, GATHER], U8, "h_scale%d" % j) for j in range(4)]
-        PER_BANK = 512 // W
-        pre = {}
+        h_codes = {(g, r): held([P, GATHER], U32, "h_codes%d%d" % (g, r)) for g in range(2) for r in range(2)}
+        h_scale = {(g, r): held([P, GATHER], U8, "h_scale%d%d" % (g, r)) for g in range(2) for r in range(2)}
         STAGE_DEPTH = 4
-        stage_ring = [held([P, 512], F32, "stage%d" % j) for j in range(STAGE_DEPTH)]
+        stage_ring = [held([P, GATHER], F32, "stage%d" % j) for j in range(STAGE_DEPTH)]
         stage_used = []
+        z_of, h_of = {}, {}
 
         def next_stage():
             stage_used.append(0)
             return stage_ring[(len(stage_used) - 1) % STAGE_DEPTH]
 
-        def inside(c):
-            g = c * W // GATHER
-            return g, slice(c * W - g * GATHER, (c + 1) * W - g * GATHER)
-
-        def first_stage(c, r):
-            g, ins = inside(c)
-            cols = slice(c * W, (c + 1) * W)
-            z = ring.tile([P, PACK, W], F32, name="z")
-            for t0 in range(0, PACK, PER_BANK):
-                pluck = psum.tile([P, PER_BANK, W], F32, name="pluck", bufs=3)
-                quill = psum.tile([P, PER_BANK, W], F32, name="quill", bufs=3)
-                for s in range(PER_BANK):
-                    m0 = (PACK * r + t0 + s) * P
+        def first_stage(g, r):
+            cols = slice(g * GATHER, (g + 1) * GATHER)
+            zt = None
+            for t in range(PACK):
+                pluck = psum.tile([P, GATHER], F32, name="pluck", bufs=3)
+                quill = psum.tile([P, GATHER], F32, name="quill", bufs=3)
+                m0 = (PACK * r + t) * P
+                nc.tensor.matmul_mx(
+                    out=quill[:],
+                    lhsT=w4_codes[:, 2 * m0:2 * (m0 + P)].bitcast(FP4X4), lhsT_scale=w4_scale[:, m0:m0 + P],
+                    rhs=v2[g].bitcast(FP8X4), rhs_scale=v2_scale[g],
+                    start=True, stop=True,
+                )
+                m = slice(t * P, (t + 1) * P)
+                for a in range(2):
                     nc.tensor.matmul_mx(
-                        out=quill[:, s, :],
-                        lhsT=w4_codes[:, 2 * m0:2 * (m0 + P)].bitcast(FP4X4), lhsT_scale=w4_scale[:, m0:m0 + P],
-                        rhs=v2[g][:, ins].bitcast(FP8X4), rhs_scale=v2_scale[g][:, ins],
-                        start=True, stop=True,
+                        out=pluck[:],
+                        lhsT=w1_codes[a, r][:, m].bitcast(FP8X4), lhsT_scale=w1_scale[a, r][:, m],
+                        rhs=v[a, g].bitcast(FP8X4), rhs_scale=v_scale[4 * a:P, cols],
+                        start=(a == 0), stop=(a == 1),
                     )
-                for s in range(PER_BANK):
-                    m = slice((t0 + s) * P, (t0 + s + 1) * P)
-                    for a in range(2):
-                        nc.tensor.matmul_mx(
-                            out=pluck[:, s, :],
-                            lhsT=w1_codes[a, r][:, m].bitcast(FP8X4), lhsT_scale=w1_scale[a, r][:, m],
-                            rhs=v[a, g][:, ins].bitcast(FP8X4), rhs_scale=v_scale[4 * a:P, cols],
-                            start=(a == 0), stop=(a == 1),
-                        )
                 quill_sb = next_stage()
-                nc.scalar.copy(quill_sb[:], quill[:].rearrange("p s n -> p (s n)"))
-                for s in range(PER_BANK):
-                    t = t0 + s
-                    nc.vector.scalar_tensor_tensor(
-                        z[:, t, :], pluck[:, s, :], stiff_sb[:, r, t:t + 1], quill_sb[:, s * W:(s + 1) * W], MULT, ADD
-                    )
-            pre[c, r] = z
+                nc.scalar.copy(quill_sb[:], quill[:])
+                if t == 0:
+                    zt = ring.tile([P, PACK, GATHER], F32, name="z", bufs=2)
+                nc.vector.scalar_tensor_tensor(zt[:, t, :], pluck[:], stiff_sb[:, r, t:t + 1], quill_sb[:], MULT, ADD)
+            z_of[g, r] = zt
 
-        def activate(c, r):
-            z = pre[c, r]
-            bent = ring.tile([P, W, PACK], F32, name="bent")
-            nc.scalar.activation(
-                bent[:].rearrange("p (m e) t -> p m t e", e=4), z[:].rearrange("p t (m e) -> p m t e", e=4), TANH
-            )
-            h = ring.tile([P, W, PACK], BF16, name="h", align_bytes=64)
-            nc.vector.tensor_tensor(h[:], bent[:], reach_sb[:, r:r + 1, :].to_broadcast([P, W, PACK]), MULT)
-            pre[c, r] = h
+        def activate_woven(g, r):
+            z = z_of[g, r]
+            h = ring.tile([P, GATHER, PACK], BF16, name="h", bufs=2, align_bytes=64)
+            for c0 in range(0, GATHER, PIECE):
+                bent = ring.tile([P, PIECE, PACK], F32, name="bent")
+                nc.scalar.activation(
+                    bent[:].rearrange("p (m e) t -> p m t e", e=4),
+                    z[:, :, c0:c0 + PIECE].rearrange("p t (m e) -> p m t e", e=4), TANH,
+                )
+                nc.vector.tensor_tensor(
+                    h[:, c0:c0 + PIECE, :], bent[:], reach_sb[:, r:r + 1, :].to_broadcast([P, PIECE, PACK]), MULT
+                )
+            h_of[g, r] = h
 
-        def quantise_h(c, r):
-            g, ins = inside(c)
-            quantise(halves[2 * g + r][:, ins], half_scales[2 * g + r][:, ins], pre[c, r][:].rearrange("p n t -> p (n t)"))
+        def activate_planes(g, r, weave_on_vector):
+            z = z_of[g, r]
+            planes = slot([P, PACK, GATHER], BF16, "planes%d" % r, "planes%d" % r)
+            for t in range(PACK):
+                bent = ring.tile([P, GATHER], F32, name="bent_plane")
+                nc.scalar.activation(bent[:], z[:, t, :], TANH)
+                nc.scalar.activation(planes[:, t, :], bent[:], COPY, scale=reach_sb[:, r, t:t + 1])
+            h = ring.tile([P, GATHER, PACK], BF16, name="h", bufs=2, align_bytes=64)
+            dst = h[:].rearrange("p (m e) t -> p m t e", e=4)
+            src = planes[:].rearrange("p t (m e) -> p m t e", e=4)
+            if weave_on_vector > 0:
+                nc.vector.tensor_copy(dst[:, :weave_on_vector], src[:, :weave_on_vector])
+            if weave_on_vector < P:
+                nc.scalar.copy(dst[:, weave_on_vector:], src[:, weave_on_vector:])
+            h_of[g, r] = h
 
-        def second_stage(g, ins, tiles, last):
+        def quantise_h(g, r):
+            quantise(h_codes[g, r][:], h_scale[g, r][:], h_of[g, r][:].rearrange("p n t -> p (n t)"))
+
+        def place(g, nt, ins, last, tag=None):
             width = ins.stop - ins.start
             j0 = g * GATHER + ins.start
-            y = psum.tile([P, 512], F32, name="y", bufs=2)
-            for s, nt in enumerate(tiles):
-                m = slice(nt * P, (nt + 1) * P)
-                for r in range(2):
-                    nc.tensor.matmul_mx(
-                        out=y[:, s * width:(s + 1) * width],
-                        lhsT=w2_codes[r][:, m].bitcast(FP8X4), lhsT_scale=w2_scale[r][:, m],
-                        rhs=halves[2 * g + r][:, ins].bitcast(FP8X4), rhs_scale=half_scales[2 * g + r][:, ins],
-                        start=(r == 0), stop=(r == 1),
-                    )
-            y_sb = next_stage()
-            nc.scalar.copy(y_sb[:, :len(tiles) * width], y[:, :len(tiles) * width])
-            for s, nt in enumerate(tiles):
-                nc.vector.tensor_tensor(
-                    page[nt][:].indirect(list3[:, j0 // 16:(j0 + width) // 16]),
-                    y_sb[:, s * width:(s + 1) * width], late["wgo"][:, j0:j0 + width], MULT,
+            y = psum.tile([P, GATHER], F32, name="y", bufs=2)
+            m = slice(nt * P, (nt + 1) * P)
+            for r in range(2):
+                nc.tensor.matmul_mx(
+                    out=y[:, :width],
+                    lhsT=w2_codes[r][:, m].bitcast(FP8X4), lhsT_scale=w2_scale[r][:, m],
+                    rhs=h_codes[g, r][:, ins].bitcast(FP8X4), rhs_scale=h_scale[g, r][:, ins],
+                    start=(r == 0), stop=(r == 1),
                 )
-                if last:
-                    nc.sync.dma_start(out[nt * P:(nt + 1) * P, :], page[nt][:])
+            y_sb = ring.tile([P, GATHER], F32, name="y_sb") if tag is None else slot([P, width], F32, "y_tail", tag)
+            nc.scalar.copy(y_sb[:, :width], y[:, :width])
+            nc.vector.tensor_tensor(
+                page[nt][:].indirect(list3[:, j0 // 16:(j0 + width) // 16]),
+                y_sb[:, :width], late["wgo"][:, j0:j0 + width], MULT,
+            )
+            if last:
+                nc.sync.dma_start(out[nt * P:(nt + 1) * P, :], page[nt][:])
 
-        def place(c, nt, last=False):
-            g, ins = inside(c)
-            second_stage(g, ins, [nt], last)
-
-        units = [(0, 0), (1, 0), (0, 1), (1, 1), (2, 0), (2, 1), (3, 0), (3, 1)]
-        waiting = [(0, 0), (0, 1), (0, 2), (0, 3), (1, 0), (1, 1), (1, 2), (1, 3)]
-        per_step = [0, 0, 0, 0, 2, 2, 2, 2]
-        for i, unit in enumerate(units):
-            first_stage(*unit)
-            if i > 0:
-                activate(*units[i - 1])
-            if i == 0:
-                make_w1(1, 1, "w1_rounded11", 4)
-                load_page(1, "B")
-            if i == 1:
-                make_w2(0, "w2_rounded0", True)
-                load_page(2, "C")
-            if i == 2:
-                make_w2(1, "w2_rounded1", False)
-                load_page(3, "D")
-            for k in range(per_step[i]):
-                place(*waiting.pop(0))
-            if i > 0:
-                quantise_h(*units[i - 1])
-        place(2, 0)
-        activate(*units[-1])
-        quantise_h(*units[-1])
-        place(2, 1)
-        place(3, 0, True)
-        place(3, 1, True)
-        for nt in range(2, N // P):
-            second_stage(1, slice(0, GATHER), [nt], True)
+        whole = slice(0, GATHER)
+        make_w1(0, 1, "G", 1)
+        first_stage(0, 0)
+        load_w2(1, "D")
+        late["wgo"] = slot([P, S], F32, "wgo_sb", "G")
+        nc.sync.dma_start(late["wgo"][:], wgo)
+        make_w1(1, 1, "H", 1)
+        load_page(0, "B")
+        activate_woven(0, 0)
+        make_w2(0, "w2_rounded0", True)
+        load_page(1, "C")
+        load_page(2, "H")
+        first_stage(0, 1)
+        quantise_h(0, 0)
+        activate_woven(0, 1)
+        make_w2(1, "w2_rounded1", False)
+        load_page(3, "D")
+        quantise_h(0, 1)
+        first_stage(1, 0)
+        place(0, 0, whole, False)
+        first_stage(1, 1)
+        place(0, 1, whole, False)
+        activate_planes(1, 0, 0)
+        place(0, 2, whole, False)
+        place(0, 3, slice(0, PIECE), False)
+        quantise_h(1, 0)
+        activate_planes(1, 1, 128)
+        quantise_h(1, 1)
+        place(0, 3, slice(PIECE, GATHER), False, "planes1")
+        for nt in range(N // P):
+            place(1, nt, whole, True)

@@ -17,6 +17,7 @@ MULT = mybir.AluOpType.mult
 ADD = mybir.AluOpType.add
 TANH = mybir.ActivationFunctionType.Tanh
 
+OPT = {"w11":128,"sd":8,"z":4,"A":"VVVVWSSS","hl":"planes11"}
 P = 128
 PACK = 4
 PASS = P * PACK
@@ -30,6 +31,7 @@ def tile_list_plectrum_voicing_scorer_kernel(
     w1, w4_words, w4_scales, stiff, reach, w2, page1, wgo, out,
 ):
     nc = tc.nc
+    eng = {"V": nc.vector, "G": nc.gpsimd}
     with ExitStack() as ctx:
         keep = ctx.enter_context(tc.tile_pool(name="keep", bufs=1))
         ring = ctx.enter_context(tc.tile_pool(name="ring", bufs=3))
@@ -122,21 +124,30 @@ def tile_list_plectrum_voicing_scorer_kernel(
         def quantise(codes, scale, rounded):
             nc.vector.quantize_mx(out=codes.bitcast(FP8X4), scales=scale, in_=rounded)
 
-        def make_w1(a, r, tag, pieces):
+        def make_w1(a, r, tag, pieces, on_vector=0):
             rounded = keep.tile([P, PACK * PASS], BF16, name="w1_rounded%d%d" % (a, r), tag=tag, align_bytes=64)
             dst = rounded[:].rearrange("p (t m i) -> p m i t", t=PACK, i=PACK)
             src = w1_raw[a, r][:].rearrange("p i (m t) -> p m i t", t=PACK)
-            for piece in range(pieces):
-                m = slice(piece * P // pieces, (piece + 1) * P // pieces)
-                nc.scalar.copy(dst[:, m], src[:, m])
+            if on_vector > 0:
+                nc.vector.tensor_copy(dst[:, :on_vector], src[:, :on_vector])
+            if on_vector < P:
+                nc.scalar.copy(dst[:, on_vector:], src[:, on_vector:])
             quantise(w1_codes[a, r][:], w1_scale[a, r][:], rounded[:])
 
         def make_w2(r, tag, on_vector):
             rounded = keep.tile([P, PACK * N], BF16, name="w2_rounded%d" % r, tag=tag, align_bytes=64)
             dst = rounded[:].rearrange("p (m e i) -> p m i e", e=4, i=PACK)
             src = w2_raw[r][:].rearrange("p i (m e) -> p m i e", e=4)
-            if on_vector:
+            if on_vector == "V":
                 nc.vector.tensor_copy(dst, src)
+            elif on_vector == "G":
+                GP = OPT.get("GP", 4)
+                for piece in range(GP):
+                    n = slice(piece * N // GP, (piece + 1) * N // GP)
+                    nc.gpsimd.tensor_scalar(
+                        rounded[:].rearrange("p (n i) -> p n i", i=PACK)[:, n],
+                        w2_raw[r][:].rearrange("p i n -> p n i")[:, n], 1.0, 0.0, MULT, ADD,
+                    )
             else:
                 for piece in range(4):
                     m = slice(piece * P // 4, (piece + 1) * P // 4)
@@ -181,19 +192,17 @@ def tile_list_plectrum_voicing_scorer_kernel(
             w4_scale[:].rearrange("p (r t m) -> p r m t", r=2, t=PACK),
             w4s_raw[:].rearrange("p (r m t) -> p r m t", r=2, t=PACK),
         )
-        for g in range(2):
-            gather_tab2(g, "v2%d" % g)
+        gather_tab2(0, "v20")
 
-        h_codes = {(g, r): held([P, GATHER], U32, "h_codes%d%d" % (g, r)) for g in range(2) for r in range(2)}
+        h_codes = {(g, r): held([P, GATHER], U32, "h_codes%d%d" % (g, r)) for g in range(2) for r in range(2) if (g, r) != (1, 0)}
         h_scale = {(g, r): held([P, GATHER], U8, "h_scale%d%d" % (g, r)) for g in range(2) for r in range(2)}
-        STAGE_DEPTH = 4
-        stage_ring = [held([P, GATHER], F32, "stage%d" % j) for j in range(STAGE_DEPTH)]
+        STAGE_DEPTH = OPT.get("sd", 4)
         stage_used = []
         z_of, h_of = {}, {}
 
         def next_stage():
             stage_used.append(0)
-            return stage_ring[(len(stage_used) - 1) % STAGE_DEPTH]
+            return slot([P, GATHER], F32, "quill_sb", "stage%d" % ((len(stage_used) - 1) % STAGE_DEPTH))
 
         def first_stage(g, r):
             cols = slice(g * GATHER, (g + 1) * GATHER)
@@ -219,92 +228,116 @@ def tile_list_plectrum_voicing_scorer_kernel(
                 quill_sb = next_stage()
                 nc.scalar.copy(quill_sb[:], quill[:])
                 if t == 0:
-                    zt = ring.tile([P, PACK, GATHER], F32, name="z", bufs=2)
+                    zt = ring.tile([P, PACK, GATHER], F32, name="z", bufs=OPT.get("z", 2))
                 nc.vector.scalar_tensor_tensor(zt[:, t, :], pluck[:], stiff_sb[:, r, t:t + 1], quill_sb[:], MULT, ADD)
             z_of[g, r] = zt
 
-        def activate_woven(g, r):
-            z = z_of[g, r]
-            h = ring.tile([P, GATHER, PACK], BF16, name="h", bufs=2, align_bytes=64)
-            for c0 in range(0, GATHER, PIECE):
-                bent = ring.tile([P, PIECE, PACK], F32, name="bent")
-                nc.scalar.activation(
-                    bent[:].rearrange("p (m e) t -> p m t e", e=4),
-                    z[:, :, c0:c0 + PIECE].rearrange("p t (m e) -> p m t e", e=4), TANH,
-                )
-                nc.vector.tensor_tensor(
-                    h[:, c0:c0 + PIECE, :], bent[:], reach_sb[:, r:r + 1, :].to_broadcast([P, PIECE, PACK]), MULT
-                )
-            h_of[g, r] = h
+        def activate_woven(g, r, c, engine="V"):
+            z = z_of[g, r][:, :, c * PIECE:(c + 1) * PIECE]
+            h = ring.tile([P, PIECE, PACK], BF16, name="h", bufs=OPT.get("hb", 4), align_bytes=64)
+            bent = ring.tile([P, PIECE, PACK], F32, name="bent")
+            nc.scalar.activation(
+                bent[:].rearrange("p (m e) t -> p m t e", e=4), z.rearrange("p t (m e) -> p m t e", e=4), TANH,
+            )
+            eng[engine].tensor_tensor(h[:], bent[:], reach_sb[:, r:r + 1, :].to_broadcast([P, PIECE, PACK]), MULT)
+            h_of[g, r, c] = h
 
-        def activate_planes(g, r, weave_on_vector):
-            z = z_of[g, r]
-            planes = slot([P, PACK, GATHER], BF16, "planes%d" % r, "planes%d" % r)
+        def activate_planes(g, r, c, weave_on_vector):
+            z = z_of[g, r][:, :, c * PIECE:(c + 1) * PIECE]
+            planes = slot([P, PACK, PIECE], BF16, "planes", "planes%d%d" % (r, c))
+            bent = ring.tile([P, PACK, PIECE], F32, name="bent")
+            nc.scalar.activation(bent[:], z, TANH)
             for t in range(PACK):
-                bent = ring.tile([P, GATHER], F32, name="bent_plane")
-                nc.scalar.activation(bent[:], z[:, t, :], TANH)
-                nc.scalar.activation(planes[:, t, :], bent[:], COPY, scale=reach_sb[:, r, t:t + 1])
-            h = ring.tile([P, GATHER, PACK], BF16, name="h", bufs=2, align_bytes=64)
+                nc.scalar.activation(planes[:, t, :], bent[:, t, :], COPY, scale=reach_sb[:, r, t:t + 1])
+            h = ring.tile([P, PIECE, PACK], BF16, name="h", bufs=OPT.get("hb", 4), align_bytes=64)
             dst = h[:].rearrange("p (m e) t -> p m t e", e=4)
             src = planes[:].rearrange("p t (m e) -> p m t e", e=4)
-            if weave_on_vector > 0:
-                nc.vector.tensor_copy(dst[:, :weave_on_vector], src[:, :weave_on_vector])
-            if weave_on_vector < P:
-                nc.scalar.copy(dst[:, weave_on_vector:], src[:, weave_on_vector:])
-            h_of[g, r] = h
+            if weave_on_vector:
+                nc.vector.tensor_copy(dst, src)
+            else:
+                nc.scalar.copy(dst, src)
+            h_of[g, r, c] = h
 
-        def quantise_h(g, r):
-            quantise(h_codes[g, r][:], h_scale[g, r][:], h_of[g, r][:].rearrange("p n t -> p (n t)"))
+        def activate(g, r, c):
+            how = OPT.get("A", "VVVVSSSV")[4 * g + 2 * c + r]
+            if how in "VG":
+                activate_woven(g, r, c, how)
+            else:
+                activate_planes(g, r, c, how == "W")
 
-        def place(g, nt, ins, last, tag=None):
+        def quantise_h(g, r, c):
+            ins = slice(c * PIECE, (c + 1) * PIECE)
+            quantise(h_codes[g, r][:, ins], h_scale[g, r][:, ins], h_of[g, r, c][:].rearrange("p n t -> p (n t)"))
+
+        def place(g, tiles, ins, last, tag=None):
             width = ins.stop - ins.start
             j0 = g * GATHER + ins.start
             y = psum.tile([P, GATHER], F32, name="y", bufs=2)
-            m = slice(nt * P, (nt + 1) * P)
-            for r in range(2):
-                nc.tensor.matmul_mx(
-                    out=y[:, :width],
-                    lhsT=w2_codes[r][:, m].bitcast(FP8X4), lhsT_scale=w2_scale[r][:, m],
-                    rhs=h_codes[g, r][:, ins].bitcast(FP8X4), rhs_scale=h_scale[g, r][:, ins],
-                    start=(r == 0), stop=(r == 1),
+            for k, nt in enumerate(tiles):
+                m = slice(nt * P, (nt + 1) * P)
+                for r in range(2):
+                    nc.tensor.matmul_mx(
+                        out=y[:, k * width:(k + 1) * width],
+                        lhsT=w2_codes[r][:, m].bitcast(FP8X4), lhsT_scale=w2_scale[r][:, m],
+                        rhs=h_codes[g, r][:, ins].bitcast(FP8X4), rhs_scale=h_scale[g, r][:, ins],
+                        start=(r == 0), stop=(r == 1),
+                    )
+            y_sb = ring.tile([P, GATHER], F32, name="y_sb") if tag is None else slot([P, GATHER], F32, "y_held", tag)
+            nc.scalar.copy(y_sb[:], y[:])
+            for k, nt in enumerate(tiles):
+                nc.vector.tensor_tensor(
+                    page[nt][:].indirect(list3[:, j0 // 16:(j0 + width) // 16]),
+                    y_sb[:, k * width:(k + 1) * width], late["wgo"][:, j0:j0 + width], MULT,
                 )
-            y_sb = ring.tile([P, GATHER], F32, name="y_sb") if tag is None else slot([P, width], F32, "y_tail", tag)
-            nc.scalar.copy(y_sb[:, :width], y[:, :width])
-            nc.vector.tensor_tensor(
-                page[nt][:].indirect(list3[:, j0 // 16:(j0 + width) // 16]),
-                y_sb[:, :width], late["wgo"][:, j0:j0 + width], MULT,
-            )
-            if last:
-                nc.sync.dma_start(out[nt * P:(nt + 1) * P, :], page[nt][:])
+                if last:
+                    nc.sync.dma_start(out[nt * P:(nt + 1) * P, :], page[nt][:])
 
         whole = slice(0, GATHER)
+        W2 = OPT.get("W2", "GG")
         make_w1(0, 1, "G", 1)
         first_stage(0, 0)
         load_w2(1, "D")
         late["wgo"] = slot([P, S], F32, "wgo_sb", "G")
         nc.sync.dma_start(late["wgo"][:], wgo)
-        make_w1(1, 1, "H", 1)
+        make_w1(1, 1, "H", 1, OPT.get("w11", 0))
+        gather_tab2(1, "H")
         load_page(0, "B")
-        activate_woven(0, 0)
-        make_w2(0, "w2_rounded0", True)
-        load_page(1, "C")
-        load_page(2, "H")
         first_stage(0, 1)
-        quantise_h(0, 0)
-        activate_woven(0, 1)
-        make_w2(1, "w2_rounded1", False)
+        lo, hi = slice(0, PIECE), slice(PIECE, GATHER)
+        activate(0, 0, 0)
+        activate(0, 0, 1)
+        if OPT.get("o1", 0) == 0:
+            first_stage(1, 0)
+        make_w2(0, "w2_rounded0", W2[0])
+        load_page(1, "C")
+        load_page(2, "A")
+        quantise_h(0, 0, 0)
+        quantise_h(0, 0, 1)
+        activate(0, 1, 0)
+        activate(0, 1, 1)
+        make_w2(1, "w2_rounded1", W2[1])
         load_page(3, "D")
-        quantise_h(0, 1)
-        first_stage(1, 0)
-        place(0, 0, whole, False)
+        quantise_h(0, 1, 0)
+        quantise_h(0, 1, 1)
+        if OPT.get("o1", 0) == 1:
+            first_stage(1, 0)
         first_stage(1, 1)
-        place(0, 1, whole, False)
-        activate_planes(1, 0, 0)
-        place(0, 2, whole, False)
-        place(0, 3, slice(0, PIECE), False)
-        quantise_h(1, 0)
-        activate_planes(1, 1, 128)
-        quantise_h(1, 1)
-        place(0, 3, slice(PIECE, GATHER), False, "planes1")
-        for nt in range(N // P):
-            place(1, nt, whole, True)
+        first_tag = "stage%d" % (OPT.get("h0", 13) % STAGE_DEPTH) if "h0" in OPT else "y00"
+        place(0, [0], whole, False, first_tag)
+        h_codes[1, 0] = slot([P, GATHER], U32, "h_codes10", first_tag)
+        seq = [(0, 0), (1, 0), (0, 1), (1, 1)] if OPT.get("o2", 0) == 0 else [(0, 0), (0, 1), (1, 0), (1, 1)]
+        activate(1, *seq[0])
+        place(0, [1], whole, False, "stage%d" % (OPT.get("h1", 15) % STAGE_DEPTH) if "h1" in OPT else None)
+        activate(1, *seq[1])
+        quantise_h(1, *seq[0])
+        place(0, [2], whole, False)
+        quantise_h(1, *seq[1])
+        activate(1, *seq[2])
+        place(0, [3], whole, False)
+        activate(1, *seq[3])
+        quantise_h(1, *seq[2])
+        quantise_h(1, *seq[3])
+        place(1, [0, 1], lo, False, OPT.get("hl", "planes11"))
+        place(1, [0, 1], hi, True)
+        place(1, [2], whole, True)
+        place(1, [3], whole, True)

from contextlib import ExitStack

import concourse.mybir as mybir

K, K2, H, N, T, S, T2 = 1024, 512, 1024, 512, 2048, 1024, 2048
FLOPS = 2 * S * H * (K + K2 + N)

F32 = mybir.dt.float32
BF16 = mybir.dt.bfloat16
I32 = mybir.dt.int32
U32 = mybir.dt.uint32
U16 = mybir.dt.uint16
U8 = mybir.dt.uint8
FP8X4 = mybir.dt.float8_e4m3fn_x4
FP4X4 = mybir.dt.float4_e2m1fn_x4
MULT = mybir.AluOpType.mult
ADD = mybir.AluOpType.add
TANH = mybir.ActivationFunctionType.Tanh

OPT = {"w11":128,"sd":8,"z":4,"A":"VVVVWSSS","hl":"planes11"}
P = 128
PACK = 4
PASS = P * PACK
GATHER = 512
PIECE = 256
COPY = mybir.ActivationFunctionType.Copy


def tile_list_plectrum_voicing_scorer_kernel(
    tc, tab_words, tab_scales, tab2_words, tab2_scales, offs, offs2, offs3,
    w1, w4_words, w4_scales, stiff, reach, w2, page1, wgo, out,
):
    nc = tc.nc
    eng = {"V": nc.vector, "G": nc.gpsimd}
    with ExitStack() as ctx:
        keep = ctx.enter_context(tc.tile_pool(name="keep", bufs=1))
        ring = ctx.enter_context(tc.tile_pool(name="ring", bufs=3))
        psum = ctx.enter_context(tc.psum_pool(name="psum", bufs=1))

        def held(shape, dtype, name):
            return keep.tile(shape, dtype, name=name, align_bytes=64)

        list1 = keep.tile([P, S // 16], U16, name="list1")
        list2 = keep.tile([P, S // 16], U16, name="list2")
        list3 = keep.tile([P, S // 16], U16, name="list3")
        def slot(shape, dtype, name, tag):
            return keep.tile(shape, dtype, name=name, tag=tag, align_bytes=64)

        tab_sb = [held([P, T], I32, "tab_sb0"), slot([P, T], I32, "tab_sb1", "B")]
        tabs_sb = held([P, T], U8, "tabs_sb")
        w4_raw = held([P, 2 * H], U8, "w4_raw")
        tab2s_sb = held([P, T], U8, "tab2s_sb")
        w4s_raw = held([P, H], U8, "w4s_raw")
        w1_raw, w2_raw, page, late = {}, {}, {}, {}
        stiff_sb = held([P, 2, PACK], F32, "stiff_sb")
        reach_sb = held([P, 2, PACK], F32, "reach_sb")

        def words(dram):
            return dram.rearrange("p t i -> p (t i)").bitcast(I32)

        def load_w2(r, tag):
            w2_raw[r] = slot([P, PACK, N], F32, "w2_raw%d" % r, tag)
            nc.sync.dma_start(w2_raw[r][:], w2[r * PASS:(r + 1) * PASS, :].rearrange("(p i) n -> p i n", i=PACK))

        def load_page(nt, tag):
            page[nt] = slot([P, T2], F32, "page%d" % nt, tag)
            nc.sync.dma_start(page[nt][:], page1[nt * P:(nt + 1) * P, :])

        def load_w1(a, r, tag):
            w1_raw[a, r] = slot([P, PACK, PASS], F32, "w1_raw%d%d" % (a, r), tag)
            nc.sync.dma_start(
                w1_raw[a, r][:],
                w1[a * PASS:(a + 1) * PASS, r * PASS:(r + 1) * PASS].rearrange("(p i) c -> p i c", i=PACK),
            )

        def load_scale_rows(plane, rows):
            nc.vector.memset(plane[:].bitcast(I32), 0)
            for q in range(4):
                nc.sync.dma_start(plane[32 * q:32 * q + 4, :].bitcast(I32), rows[4 * q:4 * q + 4, :].bitcast(I32))

        nc.sync.dma_start(list1[:], offs)
        nc.sync.dma_start(tab_sb[0][:], words(tab_words[0]))
        nc.sync.dma_start(w4_raw[:].bitcast(I32), w4_words[0].bitcast(I32))
        nc.sync.dma_start(list2[:], offs2)
        nc.sync.dma_start(list3[:], offs3)
        nc.sync.dma_start(stiff_sb[:], stiff.rearrange("(r p t) -> p r t", p=P, t=PACK))
        nc.sync.dma_start(reach_sb[:], reach.rearrange("(r p t) -> p r t", p=P, t=PACK))
        load_w1(0, 0, "A")
        nc.vector.memset(tabs_sb[:].bitcast(I32), 0)
        for a in range(2):
            for e in range(2):
                nc.sync.dma_start(tabs_sb[4 * a + e:P:16, :].bitcast(I32), tab_scales[a, e:16:2, :].bitcast(I32))
        nc.sync.dma_start(tab_sb[1][:], words(tab_words[1]))
        load_scale_rows(tab2s_sb, tab2_scales[0])
        load_w1(1, 0, "C")
        load_scale_rows(w4s_raw, w4_scales[0])
        load_w1(0, 1, "D")

        vs_picked = held([P, S], U8, "vs_picked")
        v_scale = held([P, S], U8, "v_scale")
        v_first = held([P, S], U32, "v_first")
        v = {(0, g): v_first[:, g * GATHER:(g + 1) * GATHER] for g in range(2)}
        v2, v2_scale = {}, {}

        def gather(dst, window, offsets, g):
            cols = slice(g * GATHER // 16, (g + 1) * GATHER // 16)
            nc.vector.tensor_copy(dst, window.indirect(offsets[:, cols]))

        w4_codes = held([P, 2 * H], U8, "w4_codes")
        w4_scale = held([P, H], U8, "w4_scale")
        nc.vector.tensor_copy(
            w4_codes[:].bitcast(U16).rearrange("p (r t m) -> p r m t", r=2, t=PACK),
            w4_raw[:].bitcast(U16).rearrange("p (r m t) -> p r m t", r=2, t=PACK),
        )
        nc.vector.tensor_copy(v_first[:], tab_sb[0][:].bitcast(U32).indirect(list1[:]))
        nc.vector.tensor_copy(vs_picked[:], tabs_sb[:].indirect(list1[:]))
        nc.vector.tensor_copy(v_scale[:].bitcast(I32), vs_picked[:].bitcast(I32))

        w1_codes = {(a, r): held([P, PASS], U32, "w1_codes%d%d" % (a, r)) for a in range(2) for r in range(2)}
        w1_scale = {(a, r): held([P, PASS], U8, "w1_scale%d%d" % (a, r)) for a in range(2) for r in range(2)}
        w2_codes = [held([P, N], U32, "w2_codes%d" % r) for r in range(2)]
        w2_scale = [held([P, N], U8, "w2_scale%d" % r) for r in range(2)]

        def quantise(codes, scale, rounded):
            nc.vector.quantize_mx(out=codes.bitcast(FP8X4), scales=scale, in_=rounded)

        def make_w1(a, r, tag, pieces, on_vector=0):
            rounded = keep.tile([P, PACK * PASS], BF16, name="w1_rounded%d%d" % (a, r), tag=tag, align_bytes=64)
            dst = rounded[:].rearrange("p (t m i) -> p m i t", t=PACK, i=PACK)
            src = w1_raw[a, r][:].rearrange("p i (m t) -> p m i t", t=PACK)
            if on_vector > 0:
                nc.vector.tensor_copy(dst[:, :on_vector], src[:, :on_vector])
            if on_vector < P:
                nc.scalar.copy(dst[:, on_vector:], src[:, on_vector:])
            quantise(w1_codes[a, r][:], w1_scale[a, r][:], rounded[:])

        def make_w2(r, tag, on_vector):
            rounded = keep.tile([P, PACK * N], BF16, name="w2_rounded%d" % r, tag=tag, align_bytes=64)
            dst = rounded[:].rearrange("p (m e i) -> p m i e", e=4, i=PACK)
            src = w2_raw[r][:].rearrange("p i (m e) -> p m i e", e=4)
            if on_vector == "V":
                nc.vector.tensor_copy(dst, src)
            elif on_vector == "G":
                GP = OPT.get("GP", 4)
                for piece in range(GP):
                    n = slice(piece * N // GP, (piece + 1) * N // GP)
                    nc.gpsimd.tensor_scalar(
                        rounded[:].rearrange("p (n i) -> p n i", i=PACK)[:, n],
                        w2_raw[r][:].rearrange("p i n -> p n i")[:, n], 1.0, 0.0, MULT, ADD,
                    )
            else:
                for piece in range(4):
                    m = slice(piece * P // 4, (piece + 1) * P // 4)
                    nc.scalar.copy(dst[:, m], src[:, m])
            quantise(w2_codes[r][:], w2_scale[r][:], rounded[:])

        def gather_tab(g, tag):
            t = keep.tile([P, GATHER], U32, name="v1%d" % g, tag=tag, align_bytes=64)
            gather(t[:], tab_sb[1][:].bitcast(U32), list1, g)
            v[1, g] = t[:]

        def gather_tab2(g, tag):
            t = keep.tile([P, GATHER], U32, name="v2%d" % g, tag=tag, align_bytes=64)
            gather(t[:], tab2_sb[:].bitcast(U32), list2, g)
            v2[g] = t[:]

        def gather_tab2_scales(g, tag):
            t = keep.tile([P, GATHER], U8, name="v2_scale%d" % g, tag=tag, align_bytes=64)
            gather(t[:], tab2s_sb[:], list2, g)
            v2_scale[g] = t[:]

        make_w1(0, 0, "w1_rounded00", 1)
        for a in range(2):
            for e in range(2):
                nc.sync.dma_start(
                    v_scale[4 * a + 2 + e:P:32, :].bitcast(I32), vs_picked[16 + 4 * a + e:P:32, :].bitcast(I32)
                )
        tab2_sb = slot([P, T], I32, "tab2_sb", "A")
        nc.sync.dma_start(tab2_sb[:], words(tab2_words[0]))
        v_second = held([P, S], U32, "v_second")
        nc.vector.tensor_copy(v_second[:], tab_sb[1][:].bitcast(U32).indirect(list1[:]))
        for g in range(2):
            v[1, g] = v_second[:, g * GATHER:(g + 1) * GATHER]
        load_w1(1, 1, "B")
        v2s = held([P, S], U8, "v2s")
        nc.vector.tensor_copy(v2s[:], tab2s_sb[:].indirect(list2[:]))
        for g in range(2):
            v2_scale[g] = v2s[:, g * GATHER:(g + 1) * GATHER]
        make_w1(1, 0, "w1_rounded10", 1)
        load_w2(0, "C")
        nc.vector.tensor_copy(
            w4_scale[:].rearrange("p (r t m) -> p r m t", r=2, t=PACK),
            w4s_raw[:].rearrange("p (r m t) -> p r m t", r=2, t=PACK),
        )
        gather_tab2(0, "v20")

        h_codes = {(g, r): held([P, GATHER], U32, "h_codes%d%d" % (g, r)) for g in range(2) for r in range(2) if (g, r) != (1, 0)}
        h_scale = {(g, r): held([P, GATHER], U8, "h_scale%d%d" % (g, r)) for g in range(2) for r in range(2)}
        STAGE_DEPTH = OPT.get("sd", 4)
        stage_used = []
        z_of, h_of = {}, {}

        def next_stage():
            stage_used.append(0)
            return slot([P, GATHER], F32, "quill_sb", "stage%d" % ((len(stage_used) - 1) % STAGE_DEPTH))

        def first_stage(g, r):
            cols = slice(g * GATHER, (g + 1) * GATHER)
            zt = None
            for t in range(PACK):
                pluck = psum.tile([P, GATHER], F32, name="pluck", bufs=3)
                quill = psum.tile([P, GATHER], F32, name="quill", bufs=3)
                m0 = (PACK * r + t) * P
                nc.tensor.matmul_mx(
                    out=quill[:],
                    lhsT=w4_codes[:, 2 * m0:2 * (m0 + P)].bitcast(FP4X4), lhsT_scale=w4_scale[:, m0:m0 + P],
                    rhs=v2[g].bitcast(FP8X4), rhs_scale=v2_scale[g],
                    start=True, stop=True,
                )
                m = slice(t * P, (t + 1) * P)
                for a in range(2):
                    nc.tensor.matmul_mx(
                        out=pluck[:],
                        lhsT=w1_codes[a, r][:, m].bitcast(FP8X4), lhsT_scale=w1_scale[a, r][:, m],
                        rhs=v[a, g].bitcast(FP8X4), rhs_scale=v_scale[4 * a:P, cols],
                        start=(a == 0), stop=(a == 1),
                    )
                quill_sb = next_stage()
                nc.scalar.copy(quill_sb[:], quill[:])
                if t == 0:
                    zt = ring.tile([P, PACK, GATHER], F32, name="z", bufs=OPT.get("z", 2))
                nc.vector.scalar_tensor_tensor(zt[:, t, :], pluck[:], stiff_sb[:, r, t:t + 1], quill_sb[:], MULT, ADD)
            z_of[g, r] = zt

        def activate_woven(g, r, c, engine="V"):
            z = z_of[g, r][:, :, c * PIECE:(c + 1) * PIECE]
            h = ring.tile([P, PIECE, PACK], BF16, name="h", bufs=OPT.get("hb", 4), align_bytes=64)
            bent = ring.tile([P, PIECE, PACK], F32, name="bent")
            nc.scalar.activation(
                bent[:].rearrange("p (m e) t -> p m t e", e=4), z.rearrange("p t (m e) -> p m t e", e=4), TANH,
            )
            eng[engine].tensor_tensor(h[:], bent[:], reach_sb[:, r:r + 1, :].to_broadcast([P, PIECE, PACK]), MULT)
            h_of[g, r, c] = h

        def activate_planes(g, r, c, weave_on_vector):
            z = z_of[g, r][:, :, c * PIECE:(c + 1) * PIECE]
            planes = slot([P, PACK, PIECE], BF16, "planes", "planes%d%d" % (r, c))
            bent = ring.tile([P, PACK, PIECE], F32, name="bent")
            nc.scalar.activation(bent[:], z, TANH)
            for t in range(PACK):
                nc.scalar.activation(planes[:, t, :], bent[:, t, :], COPY, scale=reach_sb[:, r, t:t + 1])
            h = ring.tile([P, PIECE, PACK], BF16, name="h", bufs=OPT.get("hb", 4), align_bytes=64)
            dst = h[:].rearrange("p (m e) t -> p m t e", e=4)
            src = planes[:].rearrange("p t (m e) -> p m t e", e=4)
            if weave_on_vector:
                nc.vector.tensor_copy(dst, src)
            else:
                nc.scalar.copy(dst, src)
            h_of[g, r, c] = h

        def activate(g, r, c):
            how = OPT.get("A", "VVVVSSSV")[4 * g + 2 * c + r]
            if how in "VG":
                activate_woven(g, r, c, how)
            else:
                activate_planes(g, r, c, how == "W")

        def quantise_h(g, r, c):
            ins = slice(c * PIECE, (c + 1) * PIECE)
            quantise(h_codes[g, r][:, ins], h_scale[g, r][:, ins], h_of[g, r, c][:].rearrange("p n t -> p (n t)"))

        def place(g, tiles, ins, last, tag=None):
            width = ins.stop - ins.start
            j0 = g * GATHER + ins.start
            y = psum.tile([P, GATHER], F32, name="y", bufs=2)
            for k, nt in enumerate(tiles):
                m = slice(nt * P, (nt + 1) * P)
                for r in range(2):
                    nc.tensor.matmul_mx(
                        out=y[:, k * width:(k + 1) * width],
                        lhsT=w2_codes[r][:, m].bitcast(FP8X4), lhsT_scale=w2_scale[r][:, m],
                        rhs=h_codes[g, r][:, ins].bitcast(FP8X4), rhs_scale=h_scale[g, r][:, ins],
                        start=(r == 0), stop=(r == 1),
                    )
            y_sb = ring.tile([P, GATHER], F32, name="y_sb") if tag is None else slot([P, GATHER], F32, "y_held", tag)
            nc.scalar.copy(y_sb[:], y[:])
            for k, nt in enumerate(tiles):
                nc.vector.tensor_tensor(
                    page[nt][:].indirect(list3[:, j0 // 16:(j0 + width) // 16]),
                    y_sb[:, k * width:(k + 1) * width], late["wgo"][:, j0:j0 + width], MULT,
                )
                if last:
                    nc.sync.dma_start(out[nt * P:(nt + 1) * P, :], page[nt][:])

        whole = slice(0, GATHER)
        W2 = OPT.get("W2", "GG")
        make_w1(0, 1, "G", 1)
        first_stage(0, 0)
        load_w2(1, "D")
        late["wgo"] = slot([P, S], F32, "wgo_sb", "G")
        nc.sync.dma_start(late["wgo"][:], wgo)
        make_w1(1, 1, "H", 1, OPT.get("w11", 0))
        gather_tab2(1, "H")
        load_page(0, "B")
        first_stage(0, 1)
        lo, hi = slice(0, PIECE), slice(PIECE, GATHER)
        activate(0, 0, 0)
        activate(0, 0, 1)
        if OPT.get("o1", 0) == 0:
            first_stage(1, 0)
        make_w2(0, "w2_rounded0", W2[0])
        load_page(1, "C")
        load_page(2, "A")
        quantise_h(0, 0, 0)
        quantise_h(0, 0, 1)
        activate(0, 1, 0)
        activate(0, 1, 1)
        make_w2(1, "w2_rounded1", W2[1])
        load_page(3, "D")
        quantise_h(0, 1, 0)
        quantise_h(0, 1, 1)
        if OPT.get("o1", 0) == 1:
            first_stage(1, 0)
        first_stage(1, 1)
        first_tag = "stage%d" % (OPT.get("h0", 13) % STAGE_DEPTH) if "h0" in OPT else "y00"
        place(0, [0], whole, False, first_tag)
        h_codes[1, 0] = slot([P, GATHER], U32, "h_codes10", first_tag)
        seq = [(0, 0), (1, 0), (0, 1), (1, 1)] if OPT.get("o2", 0) == 0 else [(0, 0), (0, 1), (1, 0), (1, 1)]
        activate(1, *seq[0])
        place(0, [1], whole, False, "stage%d" % (OPT.get("h1", 15) % STAGE_DEPTH) if "h1" in OPT else None)
        activate(1, *seq[1])
        quantise_h(1, *seq[0])
        place(0, [2], whole, False)
        quantise_h(1, *seq[1])
        activate(1, *seq[2])
        place(0, [3], whole, False)
        activate(1, *seq[3])
        quantise_h(1, *seq[2])
        quantise_h(1, *seq[3])
        place(1, [0, 1], lo, False, OPT.get("hl", "planes11"))
        place(1, [0, 1], hi, True)
        place(1, [2], whole, True)
        place(1, [3], whole, True)
